import numpy as np
import ml_dtypes


def mxq(x, axis, fmt="e4m3"):
    dtype, down = {"e4m3": (ml_dtypes.float8_e4m3fn, 7), "e5m2": (ml_dtypes.float8_e5m2, 14)}[fmt]
    v = np.moveaxis(np.asarray(x, np.float32).astype(ml_dtypes.bfloat16).astype(np.float64), axis, -1)
    blocks = v.reshape(v.shape[:-1] + (-1, 32))
    amax = np.abs(blocks).max(-1, keepdims=True)
    byte = np.maximum(np.where(amax > 0, np.frexp(amax)[1] - 1 + 127, 0) - down, 1)
    scale = np.exp2(byte - 127.0)
    codes = (blocks / scale).astype(np.float32).astype(dtype).astype(np.float64)
    return np.moveaxis((codes * scale).reshape(v.shape), -1, axis)


WIDE = False


def mx_kscale(k):
    if not WIDE:
        return np.ones(k)
    levels = np.array([10, -10, 5, -5, 0])
    if k % 512:
        return np.exp2(np.random.permutation(np.resize(levels, k // 32))).repeat(32)
    a = np.empty((k // 512, 16))
    for p in range(k // 512):
        a[p, :8] = np.random.permutation(np.resize(levels, 8))
        for g in range(8):
            far = levels[np.abs(levels - a[p, g]) >= 10]
            a[p, g + 8] = far[np.random.randint(len(far))]
    return np.exp2(a.ravel()).repeat(32)


BF16 = ml_dtypes.bfloat16


def bf(x):
    return np.asarray(x, np.float32).astype(BF16)


def f64(x):
    return np.asarray(x).astype(np.float64)


E2M1 = np.array([0.0, 0.5, 1.0, 1.5, 2.0, 3.0, 4.0, 6.0, -0.0, -0.5, -1.0, -1.5, -2.0, -3.0, -4.0, -6.0])


def pack_weight(w, fmt):
    k, n = w.shape
    w = f64(bf(w)).reshape(k // 32, 32, n)
    amax = np.abs(w).max(1)
    if fmt == "e4m3":
        byte = np.frexp(amax)[1] - 1 + 127 - 7
    else:
        mant, ex = np.frexp(amax / 6.0)
        byte = np.where(mant > 0.5, ex, ex - 1) + 127
    byte = np.clip(np.where(amax > 0, byte, 1), 1, 254)
    scaled = (w * np.exp2(127.0 - byte)[:, None, :]).reshape(k, n).astype(np.float32)
    by_word = np.ascontiguousarray(scaled.reshape(k // 512, 128, 4, n).transpose(0, 1, 3, 2))
    if fmt == "e4m3":
        words = by_word.astype(ml_dtypes.float8_e4m3fn).view(np.uint8)
    else:
        c = by_word.astype(ml_dtypes.float4_e2m1fn).view(np.uint8) & 0xF
        words = c[..., 0::2] | (c[..., 1::2] << 4)
    return np.ascontiguousarray(words), np.ascontiguousarray(byte.astype(np.uint8).reshape(k // 512, 16, n))


def unpack_weight(words, scales, fmt):
    g, p, n, _ = words.shape
    if fmt == "e4m3":
        vals = np.ascontiguousarray(words).view(ml_dtypes.float8_e4m3fn).astype(np.float64)
    else:
        nib = np.empty((g, p, n, 4), np.uint8)
        nib[..., 0::2] = words & 0xF
        nib[..., 1::2] = words >> 4
        vals = E2M1[nib]
    vals = vals * np.repeat(np.exp2(scales.astype(np.float64) - 127.0), 8, axis=1)[..., None]
    return vals.transpose(0, 1, 3, 2).reshape(g * 512, n)
def pack4(w):
    words, scales = pack_weight(w, "e2m1")
    return words.reshape(words.shape[0], 128, -1), scales


def unpack4(words, scales):
    return unpack_weight(words.reshape(words.shape[0], 128, -1, 2), scales, "e2m1")


M, TF, TC, D, E = 1024, 1024, 2048, 1024, 1024


def draw0():
    sf, sc, u = mx_kscale(TF), mx_kscale(TC), mx_kscale(D)
    length = np.random.uniform(0.6, 1.6, M)
    pf = np.abs(np.random.standard_normal((M, TF))) / np.sqrt(TF + TC) * length[:, None]
    pc = np.abs(np.random.standard_normal((M, TC))) / np.sqrt(TF + TC) * length[:, None]
    hf = np.random.standard_normal((TF, D))
    hc = np.random.standard_normal((TC, D))
    w = np.random.standard_normal((D, E)) / np.sqrt(D)
    hc_words, hc_scales = pack4(hc / sc[:, None] * u)
    w_words, w_scales = pack4(w / u[:, None])
    return {"pf": bf(pf * sf),
            "hf": bf(hf / sf[:, None] * u),
            "pc": bf(pc * sc),
            "hc_words": hc_words, "hc_scales": hc_scales,
            "inv_len": bf(1.0 / length),
            "w_words": w_words, "w_scales": w_scales,
            "b": bf(0.3 * np.random.standard_normal(E))}


def core(pf, hf, pc, hc_words, hc_scales, inv_len, w_words, w_scales, b):
    fresh = mxq(f64(pf), 1, "e4m3") @ mxq(f64(hf), 0, "e4m3")
    cached = mxq(f64(pc), 1, "e4m3") @ unpack4(hc_words, hc_scales)
    pooled = (fresh + cached) * f64(inv_len)[:, None]
    z = mxq(pooled, 1, "e4m3") @ unpack4(w_words, w_scales)
    return np.tanh(z + f64(b))


def e4m3fn_bytes(y):
    return np.clip(np.asarray(y, np.float64), -448.0, 448.0).astype(np.float32).astype(ml_dtypes.float8_e4m3fn).view(np.uint8)


def e4m3fn_values(b):
    return np.asarray(b, np.uint8).view(ml_dtypes.float8_e4m3fn).astype(np.float64)


def setup_inputs():
    d = draw0()
    x0 = np.asarray(d['pc']).astype(np.float64)
    s = (np.max(np.abs(x0), axis=(0,), keepdims=True) / 448.0).astype(np.float32)
    out = {}
    for k, v in d.items():
        if k == 'pc':
            out['pc_bytes'] = e4m3fn_bytes(x0 / s.astype(np.float64))
            out['pc_scale'] = s
        else:
            out[k] = v
    return out


def reference(pf, hf, pc_bytes, pc_scale, hc_words, hc_scales, inv_len, w_words, w_scales, b):
    return core(pf, hf, e4m3fn_values(pc_bytes) * pc_scale.astype(np.float64), hc_words, hc_scales, inv_len, w_words, w_scales, b)

@@ -1,0 +1,418 @@
+from contextlib import ExitStack
+
+import concourse.mybir as mybir
+from concourse.masks import make_identity
+
+M, TF, TC, D, E = 1024, 1024, 2048, 1024, 1024
+FLOPS = 2 * M * D * (TF + TC) + 2 * M * D * E
+
+F32 = mybir.dt.float32
+BF16 = mybir.dt.bfloat16
+I32 = mybir.dt.int32
+U32 = mybir.dt.uint32
+U8 = mybir.dt.uint8
+FP8 = mybir.dt.float8_e4m3fn
+FP8X4 = mybir.dt.float8_e4m3fn_x4
+FP4X4 = mybir.dt.float4_e2m1fn_x4
+COPY = mybir.ActivationFunctionType.Copy
+TANH = mybir.ActivationFunctionType.Tanh
+MULT = mybir.AluOpType.mult
+ADD = mybir.AluOpType.add
+
+P = 128
+NT = M // P
+GF = TF // 512
+GC = TC // 512
+GD = D // 512
+H = 512
+
+
+def tile_pooled_sentence_embedding_s3_kernel(
+    tc, pf, hf, pc_bytes, pc_scale, hc_words, hc_scales, inv_len, w_words, w_scales, b, out
+):
+    nc = tc.nc
+    with ExitStack() as ctx:
+        keep = ctx.enter_context(tc.tile_pool(name="keep", bufs=1))
+        work = ctx.enter_context(tc.tile_pool(name="work", bufs=2))
+        psum = ctx.enter_context(tc.psum_pool(name="psum", bufs=1))
+        ctx.enter_context(tc.manual_schedule())
+
+        ident = keep.tile([P, P], F32, name="ident", align_bytes=64)
+        srows = keep.tile([P, P], F32, name="srows", align_bytes=64)
+        hc_sc = keep.tile([P, GC, D], U8, name="hc_sc", align_bytes=64)
+        w_sc = keep.tile([P, GD, E], U8, name="w_sc", align_bytes=64)
+        warm = keep.tile([P, 2], F32, name="warm", align_bytes=64)
+        nc.vector.memset(srows[:], 0.0)
+        nc.vector.memset(warm[:], 0.0)
+        nc.vector.memset(hc_sc[:].rearrange("p g n -> p (g n)").bitcast(I32), 0)
+        nc.vector.memset(w_sc[:].rearrange("p g n -> p (g n)").bitcast(I32), 0)
+        nc.scalar.activation(out=warm[:, 0:1], in_=warm[:, 1:2], func=TANH)
+        make_identity(nc, ident[:])
+
+        pcb = {}
+        pfs = {}
+
+        def load_pc(i, n):
+            t = keep.tile([P, n, TC], U8, name=f"pcb{i}", tag=f"pcb{i}", align_bytes=64)
+            nc.sync.dma_start(out=t[:], in_=pc_bytes.rearrange("(p i) k -> p i k", i=NT)[:, i : i + n, :])
+            for j in range(n):
+                pcb[i + j] = t[:, j, :]
+
+        def load_pf(i, n):
+            t = keep.tile([P, n, TF], BF16, name=f"pfs{i}", tag=f"pfs{i}", align_bytes=64)
+            nc.sync.dma_start(out=t[:], in_=pf.rearrange("(p i) k -> p i k", i=NT)[:, i : i + n, :])
+            for j in range(n):
+                pfs[i + j] = t[:, j, :]
+
+        hcw = keep.tile([P, 2, GC, 2 * H], U8, name="hcw", align_bytes=64)
+        ww = keep.tile([P, GD, 2 * E], U8, name="ww", align_bytes=64)
+        hf_raw = keep.tile([P, GF, 2, 4, H], BF16, name="hf_raw", align_bytes=64)
+        inv_b = keep.tile([P, NT], BF16, name="inv_b", align_bytes=64)
+        inv = keep.tile([P, NT], F32, name="inv", align_bytes=64)
+        bias = keep.tile([P, E], BF16, name="bias", align_bytes=64)
+
+        def load_hc(h):
+            nc.sync.dma_start(
+                out=hcw[:, h, :, :],
+                in_=hc_words.rearrange("g p n -> p g n")[:, :, 2 * H * h : 2 * H * (h + 1)],
+            )
+
+        def load_hf(g, h):
+            nc.sync.dma_start(
+                out=hf_raw[:, g, h, :, :],
+                in_=hf.rearrange("(g p t) d -> g p t d", p=P, t=4)[g, :, :, H * h : H * (h + 1)],
+            )
+
+        def load_scales(tile, src):
+            for q in range(4):
+                nc.sync.dma_start(
+                    out=tile[32 * q : 32 * q + 4, :, :].bitcast(I32),
+                    in_=src[:, 4 * q : 4 * q + 4, :].rearrange("g q n -> q g n").bitcast(I32),
+                )
+
+        nc.sync.dma_start(out=srows[0:16, :], in_=pc_scale.rearrange("o (c p) -> (o c) p", p=P))
+        load_pc(0, 1)
+        load_scales(hc_sc, hc_scales)
+        load_hc(0)
+        load_hf(0, 0)
+        load_hf(1, 0)
+        load_pf(0, 1)
+        load_pc(1, 1)
+        load_hc(1)
+        load_hf(0, 1)
+        load_hf(1, 1)
+        load_pf(1, 1)
+        nc.sync.dma_start(out=inv_b[:], in_=inv_len.rearrange("(p i) -> p i", i=NT))
+        load_pc(2, 2)
+        load_pf(2, 2)
+        load_scales(w_sc, w_scales)
+        nc.sync.dma_start(out=ww[:], in_=w_words.rearrange("g p n -> p g n"))
+        nc.sync.dma_start(out=bias[:], in_=b.partition_broadcast(P))
+        load_pc(4, 2)
+        load_pf(4, 2)
+        load_pc(6, 2)
+        load_pf(6, 2)
+
+        s_col = keep.tile([P, 16], F32, name="s_col", align_bytes=64)
+        s_all = keep.tile([P, TC], F32, name="s_all", align_bytes=64)
+        tp0 = psum.tile([P, P], F32, name="tp0", tag="t3")
+        nc.tensor.transpose(tp0[:], srows[:], ident[:])
+        nc.vector.tensor_copy(out=s_col[:], in_=tp0[:, 0:16])
+        for g in range(GC):
+            ps = psum.tile([P, 4, P], F32, name="ps_s", tag=f"t{g}")
+            for c in range(4):
+                nc.tensor.transpose(
+                    ps[:, c, :], s_col[:, 4 * g + c : 4 * g + c + 1].to_broadcast([P, P]), ident[:]
+                )
+            eng = nc.vector.tensor_copy if g == 0 else nc.scalar.copy
+            eng(out=s_all[:, 512 * g : 512 * (g + 1)], in_=ps[:].rearrange("p c n -> p (c n)"))
+
+        hfc = keep.tile([P, GF, D], U32, name="hfc", align_bytes=64)
+        hfs = keep.tile([P, GF, D], U8, name="hfs", align_bytes=64)
+        hfg = {}
+        prod, pcr, pfr = {}, {}, {}
+        tpc, gpc, qc, qs = {}, {}, {}, {}
+        tpf, gpf, fc, fs = {}, {}, {}, {}
+        acc, pooled, tpo, gpo, oc, os_ = {}, {}, {}, {}, {}, {}
+        zac, zb = {}, {}
+
+        def hf_group(g, h, engine):
+            t = work.tile([P, H, 4], BF16, name="hfg", tag=f"hfg{g}", align_bytes=64)
+            hfg[g, h] = t
+            engine(
+                out=t[:].rearrange("p (c i) t -> p c t i", i=4),
+                in_=hf_raw[:, g, h, :, :].rearrange("p t (c i) -> p c t i", i=4),
+            )
+
+        def hf_quant(g, h):
+            cols = slice(H * h, H * (h + 1))
+            nc.vector.quantize_mx(
+                out=hfc[:, g, cols].bitcast(FP8X4),
+                scales=hfs[:, g, cols],
+                in_=hfg[g, h][:].rearrange("p c t -> p (c t)"),
+            )
+
+        def product(i, g0, n):
+            if g0 == 0:
+                prod[i] = work.tile([P, TC], BF16, name="prod", tag="prod", bufs=3, align_bytes=64)
+            cols = slice(512 * g0, 512 * (g0 + n))
+            nc.vector.tensor_tensor(
+                out=prod[i][:, cols], in0=pcb[i][:, cols].bitcast(FP8), in1=s_all[:, cols], op=MULT
+            )
+
+        def reorder_pc(i):
+            t = work.tile([P, TC], BF16, name="pcr", tag="pcr", bufs=2, align_bytes=64)
+            pcr[i] = t
+            nc.vector.tensor_copy(
+                out=t[:].bitcast(F32).rearrange("m (g u p) -> m g u p", u=2, p=P),
+                in_=prod[i][:].bitcast(F32).rearrange("m (g p u) -> m g u p", u=2, p=P),
+            )
+
+        def reorder_pf(i):
+            t = work.tile([P, TF], BF16, name="pfr", tag="pfr", bufs=2, align_bytes=64)
+            pfr[i] = t
+            nc.scalar.copy(
+                out=t[:].bitcast(F32).rearrange("m (g u p) -> m g u p", u=2, p=P),
+                in_=pfs[i].bitcast(F32).rearrange("m (g p u) -> m g u p", u=2, p=P),
+            )
+
+        def words(i, ordered, plain, g, u):
+            if i in ordered:
+                return ordered[i][:].bitcast(F32)[:, 256 * g + 128 * u : 256 * g + 128 * (u + 1)]
+            return plain[i].bitcast(F32)[:, 256 * g + u : 256 * (g + 1) : 2]
+
+        def turn_pc(i, h):
+            t = psum.tile([P, 2, 2, P], F32, name="tpc", tag=f"t{1 + h}")
+            tpc[i, h] = t
+            plain = {i: prod[i][:]}
+            for g in range(2):
+                for u in range(2):
+                    nc.tensor.transpose(t[:, g, u, :], words(i, pcr, plain, 2 * h + g, u), ident[:])
+
+        def copy_pc(i, h):
+            if h == 0:
+                gpc[i] = work.tile([P, GC, P, 4], BF16, name="gpc", tag="gpc", align_bytes=64)
+            nc.scalar.copy(
+                out=gpc[i][:, 2 * h : 2 * h + 2, :, :]
+                .rearrange("p g r t -> p (g r t)")
+                .bitcast(F32)
+                .rearrange("p (g r u) -> p g r u", g=2, u=2),
+                in_=tpc[i, h][:].rearrange("p g u r -> p g r u"),
+            )
+
+        def quant_pc(i, g0, n):
+            if g0 == 0:
+                qc[i] = work.tile([P, GC * P], U32, name="qc", tag="qc", align_bytes=64)
+                qs[i] = work.tile([P, GC * P], U8, name="qs", tag="qs", align_bytes=64)
+            cols = slice(P * g0, P * (g0 + n))
+            nc.vector.quantize_mx(
+                out=qc[i][:, cols].bitcast(FP8X4),
+                scales=qs[i][:, cols],
+                in_=gpc[i][:, g0 : g0 + n, :, :].rearrange("p g r t -> p (g r t)"),
+            )
+
+        def turn_pf(i):
+            t = psum.tile([P, GF, 2, P], F32, name="tpf", tag="t0")
+            tpf[i] = t
+            for g in range(GF):
+                for u in range(2):
+                    nc.tensor.transpose(t[:, g, u, :], words(i, pfr, pfs, g, u), ident[:])
+
+        def copy_pf(i):
+            gpf[i] = work.tile([P, GF * P * 4], BF16, name="gpf", tag="gpf", align_bytes=64)
+            nc.scalar.copy(
+                out=gpf[i][:].bitcast(F32).rearrange("p (g r u) -> p g r u", g=GF, u=2),
+                in_=tpf[i][:].rearrange("p g u r -> p g r u"),
+            )
+
+        def quant_pf(i):
+            fc[i] = work.tile([P, GF * P], U32, name="fc", tag="fc", align_bytes=64)
+            fs[i] = work.tile([P, GF * P], U8, name="fs", tag="fs", align_bytes=64)
+            nc.vector.quantize_mx(out=fc[i][:].bitcast(FP8X4), scales=fs[i][:], in_=gpf[i][:])
+
+        def s1_cached(i, h):
+            acc[i, h] = psum.tile([P, H], F32, name="acc", tag="acc", bufs=4)
+            for g in range(GC):
+                rows = slice(P * g, P * (g + 1))
+                nc.tensor.matmul_mx(
+                    out=acc[i, h][:],
+                    lhsT=qc[i][:, rows].bitcast(FP8X4),
+                    lhsT_scale=qs[i][:, rows],
+                    rhs=hcw[:, h, g, :].bitcast(FP4X4),
+                    rhs_scale=hc_sc[:, g, H * h : H * (h + 1)],
+                    start=(g == 0),
+                    stop=False,
+                )
+
+        def s1_fresh(i, h):
+            for g in range(GF):
+                rows = slice(P * g, P * (g + 1))
+                nc.tensor.matmul_mx(
+                    out=acc[i, h][:],
+                    lhsT=fc[i][:, rows].bitcast(FP8X4),
+                    lhsT_scale=fs[i][:, rows],
+                    rhs=hfc[:, g, H * h : H * (h + 1)].bitcast(FP8X4),
+                    rhs_scale=hfs[:, g, H * h : H * (h + 1)],
+                    start=False,
+                    stop=(g == GF - 1),
+                )
+
+        def pool_out(i, h):
+            if h == 0:
+                pooled[i] = work.tile([P, D], BF16, name="pooled", tag="pooled", align_bytes=64)
+            nc.scalar.activation(
+                out=pooled[i][:, H * h : H * (h + 1)].rearrange("m (u p e) -> m u p e", u=2, e=2),
+                in_=acc[i, h][:].rearrange("m (p u e) -> m u p e", u=2, e=2),
+                func=COPY,
+                scale=inv[:, i : i + 1],
+            )
+
+        def turn_pooled(i):
+            t = psum.tile([P, GD, 2, P], F32, name="tpo", tag="t3")
+            tpo[i] = t
+            w = pooled[i][:].bitcast(F32)
+            for g in range(GD):
+                for u in range(2):
+                    nc.tensor.transpose(t[:, g, u, :], w[:, 256 * g + 128 * u : 256 * g + 128 * (u + 1)], ident[:])
+
+        def copy_pooled(i):
+            gpo[i] = work.tile([P, GD * P * 4], BF16, name="gpo", tag="gpo", align_bytes=64)
+            nc.scalar.copy(
+                out=gpo[i][:].bitcast(F32).rearrange("p (g r u) -> p g r u", g=GD, u=2),
+                in_=tpo[i][:].rearrange("p g u r -> p g r u"),
+            )
+
+        def quant_pooled(i):
+            oc[i] = work.tile([P, GD * P], U32, name="oc", tag="oc", align_bytes=64)
+            os_[i] = work.tile([P, GD * P], U8, name="os", tag="os", align_bytes=64)
+            nc.vector.quantize_mx(out=oc[i][:].bitcast(FP8X4), scales=os_[i][:], in_=gpo[i][:])
+
+        def s2(i, h):
+            zac[i, h] = psum.tile([P, H], F32, name="zac", tag="acc", bufs=4)
+            for g in range(GD):
+                rows = slice(P * g, P * (g + 1))
+                nc.tensor.matmul_mx(
+                    out=zac[i, h][:],
+                    lhsT=oc[i][:, rows].bitcast(FP8X4),
+                    lhsT_scale=os_[i][:, rows],
+                    rhs=ww[:, g, 2 * H * h : 2 * H * (h + 1)].bitcast(FP4X4),
+                    rhs_scale=w_sc[:, g, H * h : H * (h + 1)],
+                    start=(g == 0),
+                    stop=(g == GD - 1),
+                )
+
+        def add_bias(i, h):
+            if h == 0:
+                zb[i] = work.tile([P, E], F32, name="zb", tag="zb", bufs=3, align_bytes=64)
+            cols = slice(H * h, H * (h + 1))
+            nc.vector.tensor_tensor(out=zb[i][:, cols], in0=zac[i, h][:], in1=bias[:, cols], op=ADD)
+
+        def tanh(i, h):
+            cols = slice(H * h, H * (h + 1))
+            nc.scalar.activation(out=zb[i][:, cols], in_=zb[i][:, cols], func=TANH)
+
+        def store(i, c0, c1):
+            nc.sync.dma_start(
+                out=out.rearrange("(p i) e -> p i e", i=NT)[:, i, c0:c1], in_=zb[i][:, c0:c1]
+            )
+
+        for g in range(GC):
+            product(0, g, 1)
+        turn_pc(0, 0)
+        copy_pc(0, 0)
+        turn_pc(0, 1)
+        copy_pc(0, 1)
+        quant_pc(0, 0, 2)
+        hf_group(0, 0, nc.scalar.copy)
+        hf_group(1, 0, nc.vector.tensor_copy)
+        quant_pc(0, 2, 2)
+        turn_pf(0)
+        copy_pf(0)
+        s1_cached(0, 0)
+        product(1, 0, 2)
+        hf_quant(1, 0)
+        product(1, 2, 2)
+        turn_pc(1, 0)
+        copy_pc(1, 0)
+        turn_pc(1, 1)
+        copy_pc(1, 1)
+        s1_cached(0, 1)
+        quant_pf(0)
+        hf_quant(0, 0)
+        hf_group(0, 1, nc.vector.tensor_copy)
+        hf_group(1, 1, nc.scalar.copy)
+        s1_fresh(0, 0)
+        turn_pf(1)
+        copy_pf(1)
+        quant_pc(1, 0, 4)
+        nc.vector.tensor_copy(out=inv[:], in_=inv_b[:])
+        pool_out(0, 0)
+        quant_pf(1)
+        hf_quant(0, 1)
+        s1_cached(1, 0)
+        s1_fresh(1, 0)
+        hf_quant(1, 1)
+        product(2, 0, 2)
+        s1_fresh(0, 1)
+        s1_cached(1, 1)
+        s1_fresh(1, 1)
+        pool_out(0, 1)
+        product(2, 2, 2)
+        reorder_pc(2)
+        reorder_pf(2)
+        pool_out(1, 0)
+        pool_out(1, 1)
+
+        def period(i, first):
+            if i >= 2 and not first:
+                add_bias(i - 2, 0)
+                add_bias(i - 2, 1)
+            if i + 1 < NT:
+                turn_pf(i + 1)
+                turn_pc(i + 1, 0)
+                turn_pc(i + 1, 1)
+            turn_pooled(i - 1)
+            if i + 1 < NT:
+                copy_pf(i + 1)
+                copy_pc(i + 1, 0)
+            copy_pooled(i - 1)
+            if i + 1 < NT:
+                copy_pc(i + 1, 1)
+            if i + 2 < NT:
+                product(i + 2, 0, 2)
+            if i + 1 < NT:
+                quant_pf(i + 1)
+            if i + 2 < NT:
+                product(i + 2, 2, 2)
+            quant_pooled(i - 1)
+            if i + 2 < NT:
+                reorder_pc(i + 2)
+            if i + 1 < NT:
+                quant_pc(i + 1, 0, 4)
+            if not first and i < NT:
+                s1_cached(i, 0)
+                s1_fresh(i, 0)
+                s1_cached(i, 1)
+                s1_fresh(i, 1)
+            s2(i - 1, 0)
+            s2(i - 1, 1)
+            if i >= 2 and not first:
+                tanh(i - 2, 0)
+            if not first and i < NT:
+                pool_out(i, 0)
+            if i >= 2 and not first:
+                tanh(i - 2, 1)
+                store(i - 2, 0, E)
+            if i + 2 < NT:
+                reorder_pf(i + 2)
+            if not first and i < NT:
+                pool_out(i, 1)
+
+        period(1, True)
+        for i in range(2, NT + 1):
+            period(i, False)
+        i = NT - 1
+        for h in range(2):
+            add_bias(i, h)
+            tanh(i, h)
+            store(i, H * h, H * (h + 1))

@@ -38,11 +38,10 @@ def tile_pooled_sentence_embedding_s3_kernel(
         ctx.enter_context(tc.manual_schedule())
 
         ident = keep.tile([P, P], F32, name="ident", align_bytes=64)
-        srows = keep.tile([P, P], F32, name="srows", align_bytes=64)
+        pc_sc = keep.tile([P, GC, 4], F32, name="pc_sc", align_bytes=64)
         hc_sc = keep.tile([P, GC, D], U8, name="hc_sc", align_bytes=64)
         w_sc = keep.tile([P, GD, E], U8, name="w_sc", align_bytes=64)
         warm = keep.tile([P, 2], F32, name="warm", align_bytes=64)
-        nc.vector.memset(srows[:], 0.0)
         nc.vector.memset(warm[:], 0.0)
         nc.vector.memset(hc_sc[:].rearrange("p g n -> p (g n)").bitcast(I32), 0)
         nc.vector.memset(w_sc[:].rearrange("p g n -> p (g n)").bitcast(I32), 0)
@@ -90,21 +89,23 @@ def tile_pooled_sentence_embedding_s3_kernel(
                     in_=src[:, 4 * q : 4 * q + 4, :].rearrange("g q n -> q g n").bitcast(I32),
                 )
 
-        nc.sync.dma_start(out=srows[0:16, :], in_=pc_scale.rearrange("o (c p) -> (o c) p", p=P))
         load_pc(0, 1)
+        nc.sync.dma_start(out=pc_sc[:], in_=pc_scale.rearrange("o (g p t) -> p (o g) t", p=P, t=4))
+        nc.sync.dma_start(out=inv_b[:], in_=inv_len.rearrange("(p i) -> p i", i=NT))
         load_scales(hc_sc, hc_scales)
         load_hc(0)
         load_hf(0, 0)
+        load_pc(1, 1)
         load_hf(1, 0)
         load_pf(0, 1)
-        load_pc(1, 1)
         load_hc(1)
         load_hf(0, 1)
+        load_pc(2, 1)
         load_hf(1, 1)
         load_pf(1, 1)
-        nc.sync.dma_start(out=inv_b[:], in_=inv_len.rearrange("(p i) -> p i", i=NT))
-        load_pc(2, 2)
-        load_pf(2, 2)
+        load_pf(2, 1)
+        load_pc(3, 1)
+        load_pf(3, 1)
         load_scales(w_sc, w_scales)
         nc.sync.dma_start(out=ww[:], in_=w_words.rearrange("g p n -> p g n"))
         nc.sync.dma_start(out=bias[:], in_=b.partition_broadcast(P))
@@ -113,24 +114,10 @@ def tile_pooled_sentence_embedding_s3_kernel(
         load_pc(6, 2)
         load_pf(6, 2)
 
-        s_col = keep.tile([P, 16], F32, name="s_col", align_bytes=64)
-        s_all = keep.tile([P, TC], F32, name="s_all", align_bytes=64)
-        tp0 = psum.tile([P, P], F32, name="tp0", tag="t3")
-        nc.tensor.transpose(tp0[:], srows[:], ident[:])
-        nc.vector.tensor_copy(out=s_col[:], in_=tp0[:, 0:16])
-        for g in range(GC):
-            ps = psum.tile([P, 4, P], F32, name="ps_s", tag=f"t{g}")
-            for c in range(4):
-                nc.tensor.transpose(
-                    ps[:, c, :], s_col[:, 4 * g + c : 4 * g + c + 1].to_broadcast([P, P]), ident[:]
-                )
-            eng = nc.vector.tensor_copy if g == 0 else nc.scalar.copy
-            eng(out=s_all[:, 512 * g : 512 * (g + 1)], in_=ps[:].rearrange("p c n -> p (c n)"))
-
         hfc = keep.tile([P, GF, D], U32, name="hfc", align_bytes=64)
         hfs = keep.tile([P, GF, D], U8, name="hfs", align_bytes=64)
         hfg = {}
-        prod, pcr, pfr = {}, {}, {}
+        wide, pcr, pfr = {}, {}, {}
         tpc, gpc, qc, qs = {}, {}, {}, {}
         tpf, gpf, fc, fs = {}, {}, {}, {}
         acc, pooled, tpo, gpo, oc, os_ = {}, {}, {}, {}, {}, {}
@@ -152,20 +139,18 @@ def tile_pooled_sentence_embedding_s3_kernel(
                 in_=hfg[g, h][:].rearrange("p c t -> p (c t)"),
             )
 
-        def product(i, g0, n):
+        def widen(i, g0, n, engine):
             if g0 == 0:
-                prod[i] = work.tile([P, TC], BF16, name="prod", tag="prod", bufs=3, align_bytes=64)
+                wide[i] = work.tile([P, TC], BF16, name="wide", tag="wide", bufs=3, align_bytes=64)
             cols = slice(512 * g0, 512 * (g0 + n))
-            nc.vector.tensor_tensor(
-                out=prod[i][:, cols], in0=pcb[i][:, cols].bitcast(FP8), in1=s_all[:, cols], op=MULT
-            )
+            engine(out=wide[i][:, cols], in_=pcb[i][:, cols].bitcast(FP8))
 
         def reorder_pc(i):
             t = work.tile([P, TC], BF16, name="pcr", tag="pcr", bufs=2, align_bytes=64)
             pcr[i] = t
-            nc.vector.tensor_copy(
+            nc.scalar.copy(
                 out=t[:].bitcast(F32).rearrange("m (g u p) -> m g u p", u=2, p=P),
-                in_=prod[i][:].bitcast(F32).rearrange("m (g p u) -> m g u p", u=2, p=P),
+                in_=wide[i][:].bitcast(F32).rearrange("m (g p u) -> m g u p", u=2, p=P),
             )
 
         def reorder_pf(i):
@@ -184,21 +169,22 @@ def tile_pooled_sentence_embedding_s3_kernel(
         def turn_pc(i, h):
             t = psum.tile([P, 2, 2, P], F32, name="tpc", tag=f"t{1 + h}")
             tpc[i, h] = t
-            plain = {i: prod[i][:]}
+            plain = {i: wide[i][:]}
             for g in range(2):
                 for u in range(2):
                     nc.tensor.transpose(t[:, g, u, :], words(i, pcr, plain, 2 * h + g, u), ident[:])
 
-        def copy_pc(i, h):
+        def product(i, h):
             if h == 0:
                 gpc[i] = work.tile([P, GC, P, 4], BF16, name="gpc", tag="gpc", align_bytes=64)
-            nc.scalar.copy(
-                out=gpc[i][:, 2 * h : 2 * h + 2, :, :]
-                .rearrange("p g r t -> p (g r t)")
-                .bitcast(F32)
-                .rearrange("p (g r u) -> p g r u", g=2, u=2),
-                in_=tpc[i, h][:].rearrange("p g u r -> p g r u"),
-            )
+            for j in range(2):
+                g = 2 * h + j
+                nc.vector.tensor_tensor(
+                    out=gpc[i][:, g, :, :].rearrange("p r (u e) -> p r u e", u=2),
+                    in0=tpc[i, h][:, j, :, :].bitcast(BF16).rearrange("p u (r e) -> p r u e", e=2),
+                    in1=pc_sc[:, g, :].rearrange("p (u e) -> p u e", u=2).unsqueeze(1).to_broadcast([P, P, 2, 2]),
+                    op=MULT,
+                )
 
         def quant_pc(i, g0, n):
             if g0 == 0:
@@ -316,103 +302,122 @@ def tile_pooled_sentence_embedding_s3_kernel(
                 out=out.rearrange("(p i) e -> p i e", i=NT)[:, i, c0:c1], in_=zb[i][:, c0:c1]
             )
 
-        for g in range(GC):
-            product(0, g, 1)
+        widen(0, 0, 1, nc.vector.tensor_copy)
+        widen(0, 1, 1, nc.vector.tensor_copy)
+        widen(0, 2, 1, nc.scalar.copy)
+        widen(0, 3, 1, nc.vector.tensor_copy)
         turn_pc(0, 0)
-        copy_pc(0, 0)
         turn_pc(0, 1)
-        copy_pc(0, 1)
-        quant_pc(0, 0, 2)
+        for g in range(GC):
+            widen(1, g, 1, nc.gpsimd.tensor_copy)
+        product(0, 0)
+        product(0, 1)
         hf_group(0, 0, nc.scalar.copy)
-        hf_group(1, 0, nc.vector.tensor_copy)
+        quant_pc(0, 0, 2)
         quant_pc(0, 2, 2)
+        nc.vector.tensor_copy(out=inv[:], in_=inv_b[:])
+        s1_cached(0, 0)
+        turn_pc(1, 0)
+        turn_pc(1, 1)
         turn_pf(0)
         copy_pf(0)
-        s1_cached(0, 0)
-        product(1, 0, 2)
-        hf_quant(1, 0)
-        product(1, 2, 2)
-        turn_pc(1, 0)
-        copy_pc(1, 0)
-        turn_pc(1, 1)
-        copy_pc(1, 1)
+        hf_group(1, 0, nc.vector.tensor_copy)
+        for i in (2, 3):
+            for g in range(GC):
+                widen(i, g, 1, nc.gpsimd.tensor_copy)
+        hf_group(0, 1, nc.scalar.copy)
         s1_cached(0, 1)
-        quant_pf(0)
+        product(1, 0)
         hf_quant(0, 0)
-        hf_group(0, 1, nc.vector.tensor_copy)
-        hf_group(1, 1, nc.scalar.copy)
+        hf_quant(1, 0)
+        product(1, 1)
+        quant_pf(0)
         s1_fresh(0, 0)
         turn_pf(1)
         copy_pf(1)
-        quant_pc(1, 0, 4)
-        nc.vector.tensor_copy(out=inv[:], in_=inv_b[:])
         pool_out(0, 0)
+        quant_pc(1, 0, 4)
+        hf_group(1, 1, nc.vector.tensor_copy)
         quant_pf(1)
-        hf_quant(0, 1)
         s1_cached(1, 0)
         s1_fresh(1, 0)
+        pool_out(1, 0)
+        turn_pc(2, 0)
+        turn_pc(2, 1)
+        turn_pf(2)
+        copy_pf(2)
+        hf_quant(0, 1)
         hf_quant(1, 1)
-        product(2, 0, 2)
         s1_fresh(0, 1)
         s1_cached(1, 1)
         s1_fresh(1, 1)
         pool_out(0, 1)
-        product(2, 2, 2)
-        reorder_pc(2)
-        reorder_pf(2)
-        pool_out(1, 0)
-        pool_out(1, 1)
+        turn_pooled(0)
+        product(2, 0)
+        product(2, 1)
+        quant_pc(2, 0, 2)
+        quant_pc(2, 2, 2)
+        quant_pf(2)
+        copy_pooled(0)
+        quant_pooled(0)
+        reorder_pf(3)
+        reorder_pc(3)
 
-        def period(i, first):
-            if i >= 2 and not first:
-                add_bias(i - 2, 0)
-                add_bias(i - 2, 1)
-            if i + 1 < NT:
-                turn_pf(i + 1)
-                turn_pc(i + 1, 0)
-                turn_pc(i + 1, 1)
-            turn_pooled(i - 1)
-            if i + 1 < NT:
-                copy_pf(i + 1)
-                copy_pc(i + 1, 0)
-            copy_pooled(i - 1)
-            if i + 1 < NT:
-                copy_pc(i + 1, 1)
-            if i + 2 < NT:
-                product(i + 2, 0, 2)
-            if i + 1 < NT:
-                quant_pf(i + 1)
-            if i + 2 < NT:
-                product(i + 2, 2, 2)
-            quant_pooled(i - 1)
-            if i + 2 < NT:
-                reorder_pc(i + 2)
-            if i + 1 < NT:
-                quant_pc(i + 1, 0, 4)
-            if not first and i < NT:
+        def there(i):
+            return 0 <= i < NT
+
+        def period(i):
+            if there(i):
                 s1_cached(i, 0)
                 s1_fresh(i, 0)
+            if there(i - 1):
+                pool_out(i - 1, 1)
+            if there(i - 3):
+                for h in range(2):
+                    add_bias(i - 3, h)
+                    tanh(i - 3, h)
+                store(i - 3, 0, E)
+            if there(i + 1):
+                turn_pc(i + 1, 0)
+            if there(i - 1):
+                turn_pooled(i - 1)
+            if there(i + 1):
+                turn_pc(i + 1, 1)
+                turn_pf(i + 1)
+            if there(i - 1):
+                copy_pooled(i - 1)
+            if there(i + 1):
+                copy_pf(i + 1)
+            if there(i):
+                pool_out(i, 0)
+            if there(i + 1):
+                product(i + 1, 0)
+                product(i + 1, 1)
+            if there(i - 1):
+                quant_pooled(i - 1)
+            if there(i + 1):
+                quant_pc(i + 1, 0, 2)
+                quant_pc(i + 1, 2, 2)
+                quant_pf(i + 1)
+            if there(i):
                 s1_cached(i, 1)
                 s1_fresh(i, 1)
-            s2(i - 1, 0)
-            s2(i - 1, 1)
-            if i >= 2 and not first:
-                tanh(i - 2, 0)
-            if not first and i < NT:
-                pool_out(i, 0)
-            if i >= 2 and not first:
-                tanh(i - 2, 1)
-                store(i - 2, 0, E)
-            if i + 2 < NT:
-                reorder_pf(i + 2)
-            if not first and i < NT:
-                pool_out(i, 1)
+            for h in range(2):
+                s2(i - 2, h)
+            if there(i + 2):
+                for g in range(GC):
+                    if i + 2 > 3:
+                        widen(i + 2, g, 1, nc.gpsimd.tensor_copy)
+                if i + 2 > 3:
+                    reorder_pf(i + 2)
+                    reorder_pc(i + 2)
 
-        period(1, True)
         for i in range(2, NT + 1):
-            period(i, False)
-        i = NT - 1
+            period(i)
         for h in range(2):
-            add_bias(i, h)
-            tanh(i, h)
-            store(i, H * h, H * (h + 1))
+            s2(NT - 1, h)
+        for i in (NT - 2, NT - 1):
+            for h in range(2):
+                add_bias(i, h)
+                tanh(i, h)
+                store(i, H * h, H * (h + 1))

@@ -25,6 +25,7 @@ GF = TF // 512
 GC = TC // 512
 GD = D // 512
 H = 512
+XT = 4
 
 
 def tile_pooled_sentence_embedding_s3_kernel(
@@ -43,6 +44,8 @@ def tile_pooled_sentence_embedding_s3_kernel(
         w_sc = keep.tile([P, GD, E], U8, name="w_sc", align_bytes=64)
         warm = keep.tile([P, 2], F32, name="warm", align_bytes=64)
         nc.vector.memset(warm[:], 0.0)
+        idle = keep.tile([P, H], BF16, name="idle", align_bytes=64)
+        nc.gpsimd.memset(idle[:], 0.0)
         nc.vector.memset(hc_sc[:].rearrange("p g n -> p (g n)").bitcast(I32), 0)
         nc.vector.memset(w_sc[:].rearrange("p g n -> p (g n)").bitcast(I32), 0)
         nc.scalar.activation(out=warm[:, 0:1], in_=warm[:, 1:2], func=TANH)
@@ -63,6 +66,7 @@ def tile_pooled_sentence_embedding_s3_kernel(
             for j in range(n):
                 pfs[i + j] = t[:, j, :]
 
+        s_all = keep.tile([P, TC], F32, name="s_all", align_bytes=64)
         hcw = keep.tile([P, 2, GC, 2 * H], U8, name="hcw", align_bytes=64)
         ww = keep.tile([P, GD, 2 * E], U8, name="ww", align_bytes=64)
         hf_raw = keep.tile([P, GF, 2, 4, H], BF16, name="hf_raw", align_bytes=64)
@@ -89,30 +93,31 @@ def tile_pooled_sentence_embedding_s3_kernel(
                     in_=src[:, 4 * q : 4 * q + 4, :].rearrange("g q n -> q g n").bitcast(I32),
                 )
 
-        load_pc(0, 1)
-        nc.sync.dma_start(out=pc_sc[:], in_=pc_scale.rearrange("o (g p t) -> p (o g) t", p=P, t=4))
-        nc.sync.dma_start(out=inv_b[:], in_=inv_len.rearrange("(p i) -> p i", i=NT))
-        load_scales(hc_sc, hc_scales)
-        load_hc(0)
-        load_hf(0, 0)
         load_pc(1, 1)
+        nc.sync.dma_start(out=pc_sc[:], in_=pc_scale.rearrange("o (g p t) -> p (o g) t", p=P, t=4))
+        load_pc(0, 1)
+        nc.sync.dma_start(out=inv_b[:], in_=inv_len.rearrange("(p i) -> p i", i=NT))
+        load_hf(0, 0)
+        load_hf(0, 1)
         load_hf(1, 0)
         load_pf(0, 1)
-        load_hc(1)
-        load_hf(0, 1)
-        load_pc(2, 1)
-        load_hf(1, 1)
+        load_scales(hc_sc, hc_scales)
+        load_hc(0)
+        load_pf(3, 1)
         load_pf(1, 1)
         load_pf(2, 1)
-        load_pc(3, 1)
-        load_pf(3, 1)
+        load_hc(1)
+        load_pc(2, 1)
+        load_hf(1, 1)
+        load_pc(4, 2)
         load_scales(w_sc, w_scales)
+        load_pc(3, 1)
+        nc.sync.dma_start(out=s_all[:], in_=pc_scale.rearrange("o k -> (o k)").partition_broadcast(P))
+        load_pf(4, 2)
         nc.sync.dma_start(out=ww[:], in_=w_words.rearrange("g p n -> p g n"))
         nc.sync.dma_start(out=bias[:], in_=b.partition_broadcast(P))
-        load_pc(4, 2)
-        load_pf(4, 2)
-        load_pc(6, 2)
         load_pf(6, 2)
+        load_pc(6, 2)
 
         hfc = keep.tile([P, GF, D], U32, name="hfc", align_bytes=64)
         hfs = keep.tile([P, GF, D], U8, name="hfs", align_bytes=64)
@@ -145,13 +150,47 @@ def tile_pooled_sentence_embedding_s3_kernel(
             cols = slice(512 * g0, 512 * (g0 + n))
             engine(out=wide[i][:, cols], in_=pcb[i][:, cols].bitcast(FP8))
 
+        def scale_rows(i, g0, n):
+            if g0 == 0:
+                wide[i] = work.tile([P, TC], BF16, name="wide", tag="wide", bufs=3, align_bytes=64)
+            cols = slice(512 * g0, 512 * (g0 + n))
+            nc.vector.tensor_tensor(
+                out=wide[i][:, cols], in0=pcb[i][:, cols].bitcast(FP8), in1=s_all[:, cols], op=MULT
+            )
+
         def reorder_pc(i):
             t = work.tile([P, TC], BF16, name="pcr", tag="pcr", bufs=2, align_bytes=64)
             pcr[i] = t
-            nc.scalar.copy(
+            nc.vector.tensor_copy(
                 out=t[:].bitcast(F32).rearrange("m (g u p) -> m g u p", u=2, p=P),
                 in_=wide[i][:].bitcast(F32).rearrange("m (g p u) -> m g u p", u=2, p=P),
             )
+
+        def copy_pc(i, h):
+            if h == 0:
+                gpc[i] = work.tile([P, GC, P, 4], BF16, name="gpc", tag="gpc", align_bytes=64)
+            nc.scalar.copy(
+                out=gpc[i][:, 2 * h : 2 * h + 2, :, :]
+                .rearrange("p g r t -> p (g r t)")
+                .bitcast(F32)
+                .rearrange("p (g r u) -> p g r u", g=2, u=2),
+                in_=tpc[i, h][:].rearrange("p g u r -> p g r u"),
+            )
+
+        def keep_clock(n):
+            t = psum.tile([P, H], F32, name="clock", tag="t3")
+            for j in range(n):
+                nc.tensor.matmul(t[:], idle[:, 0:P], idle[:], start=True, stop=True)
+
+        def hf_group_gpsimd(g, h):
+            t = work.tile([P, H, 4], BF16, name="hfg", tag=f"hfg{g}", align_bytes=64)
+            hfg[g, h] = t
+            for c in range(4):
+                nc.gpsimd.tensor_scalar(
+                    t[:, P * c : P * (c + 1), :],
+                    hf_raw[:, g, h, :, P * c : P * (c + 1)].rearrange("p t d -> p d t"),
+                    1.0, 0.0, MULT, ADD,
+                )
 
         def reorder_pf(i):
             t = work.tile([P, TF], BF16, name="pfr", tag="pfr", bufs=2, align_bytes=64)
@@ -302,116 +341,134 @@ def tile_pooled_sentence_embedding_s3_kernel(
                 out=out.rearrange("(p i) e -> p i e", i=NT)[:, i, c0:c1], in_=zb[i][:, c0:c1]
             )
 
+        keep_clock(8)
         widen(0, 0, 1, nc.vector.tensor_copy)
-        widen(0, 1, 1, nc.vector.tensor_copy)
-        widen(0, 2, 1, nc.scalar.copy)
-        widen(0, 3, 1, nc.vector.tensor_copy)
+        widen(0, 1, 1, nc.scalar.copy)
+        widen(0, 2, 1, nc.vector.tensor_copy)
         turn_pc(0, 0)
-        turn_pc(0, 1)
-        for g in range(GC):
-            widen(1, g, 1, nc.gpsimd.tensor_copy)
+        keep_clock(4)
         product(0, 0)
-        product(0, 1)
-        hf_group(0, 0, nc.scalar.copy)
+        widen(1, 0, 2, nc.scalar.copy)
         quant_pc(0, 0, 2)
-        quant_pc(0, 2, 2)
-        nc.vector.tensor_copy(out=inv[:], in_=inv_b[:])
-        s1_cached(0, 0)
+        widen(0, 3, 1, nc.scalar.copy)
+        turn_pc(0, 1)
         turn_pc(1, 0)
-        turn_pc(1, 1)
+        widen(1, 2, 2, nc.scalar.copy)
+        product(0, 1)
         turn_pf(0)
-        copy_pf(0)
-        hf_group(1, 0, nc.vector.tensor_copy)
-        for i in (2, 3):
-            for g in range(GC):
-                widen(i, g, 1, nc.gpsimd.tensor_copy)
-        hf_group(0, 1, nc.scalar.copy)
-        s1_cached(0, 1)
         product(1, 0)
-        hf_quant(0, 0)
-        hf_quant(1, 0)
-        product(1, 1)
-        quant_pf(0)
-        s1_fresh(0, 0)
+        hf_group(1, 0, nc.scalar.copy)
+        copy_pf(0)
+        hf_group_gpsimd(0, 0)
+        turn_pc(1, 1)
+        quant_pc(0, 2, 2)
+        s1_cached(0, 0)
         turn_pf(1)
+        reorder_pf(3)
         copy_pf(1)
-        pool_out(0, 0)
-        quant_pc(1, 0, 4)
-        hf_group(1, 1, nc.vector.tensor_copy)
+        hf_quant(1, 0)
+        nc.vector.tensor_copy(out=inv[:], in_=inv_b[:])
+        product(1, 1)
+        widen(2, 0, 2, nc.scalar.copy)
+        s1_cached(0, 1)
+        hf_quant(0, 0)
+        quant_pf(0)
+        quant_pc(1, 0, 2)
+        hf_group(1, 1, nc.scalar.copy)
+        quant_pc(1, 2, 2)
+        turn_pf(2)
         quant_pf(1)
-        s1_cached(1, 0)
-        s1_fresh(1, 0)
-        pool_out(1, 0)
+        widen(2, 2, 2, nc.vector.tensor_copy)
+        widen(3, 0, 2, nc.scalar.copy)
         turn_pc(2, 0)
         turn_pc(2, 1)
-        turn_pf(2)
-        copy_pf(2)
-        hf_quant(0, 1)
-        hf_quant(1, 1)
-        s1_fresh(0, 1)
-        s1_cached(1, 1)
-        s1_fresh(1, 1)
-        pool_out(0, 1)
-        turn_pooled(0)
+        hf_group(0, 1, nc.vector.tensor_copy)
         product(2, 0)
-        product(2, 1)
+        s1_cached(1, 1)
+        hf_quant(0, 1)
+        s1_fresh(0, 0)
+        copy_pf(2)
+        hf_quant(1, 1)
         quant_pc(2, 0, 2)
+        product(2, 1)
+        widen(3, 2, 2, nc.vector.tensor_copy)
+        s1_cached(1, 0)
+        pool_out(0, 0)
+        s1_fresh(0, 1)
         quant_pc(2, 2, 2)
+        s1_fresh(1, 0)
+        pool_out(0, 1)
+        s1_fresh(1, 1)
+        turn_pooled(0)
         quant_pf(2)
+        pool_out(1, 0)
         copy_pooled(0)
         quant_pooled(0)
-        reorder_pf(3)
-        reorder_pc(3)
-
         def there(i):
             return 0 <= i < NT
 
         def period(i):
-            if there(i):
-                s1_cached(i, 0)
-                s1_fresh(i, 0)
             if there(i - 1):
                 pool_out(i - 1, 1)
-            if there(i - 3):
-                for h in range(2):
-                    add_bias(i - 3, h)
-                    tanh(i - 3, h)
-                store(i - 3, 0, E)
-            if there(i + 1):
-                turn_pc(i + 1, 0)
-            if there(i - 1):
-                turn_pooled(i - 1)
             if there(i + 1):
                 turn_pc(i + 1, 1)
+            if there(i + 1):
+                turn_pc(i + 1, 0)
+            if there(i + 1):
                 turn_pf(i + 1)
-            if there(i - 1):
+            if there(i + 1) and i + 1 >= XT:
+                copy_pc(i + 1, 0)
+            if there(i - 3):
+                add_bias(i - 3, 0)
+                tanh(i - 3, 0)
+            if there(i - 1) and i < NT:
+                turn_pooled(i - 1)
+            if there(i - 1) and i < NT:
                 copy_pooled(i - 1)
+            if i + 1 < XT:
+                product(i + 1, 0)
+            if there(i + 2):
+                scale_rows(i + 2, 0, 2)
+            if there(i):
+                s1_cached(i, 1)
             if there(i + 1):
                 copy_pf(i + 1)
+            if there(i - 3):
+                add_bias(i - 3, 1)
+                tanh(i - 3, 1)
+                store(i - 3, 0, E)
+            if there(i):
+                s1_cached(i, 0)
+            if i == NT:
+                turn_pooled(i - 1)
+                copy_pooled(i - 1)
+                quant_pooled(i - 1)
+            if there(i):
+                s1_fresh(i, 0)
+            if there(i + 2):
+                reorder_pf(i + 2)
+            if there(i + 2):
+                scale_rows(i + 2, 2, 2)
+            if there(i):
+                s1_fresh(i, 1)
+            if there(i - 2):
+                s2(i - 2, 0)
+            if there(i - 2):
+                s2(i - 2, 1)
+            if there(i + 1) and i + 1 >= XT:
+                copy_pc(i + 1, 1)
+            if i + 1 < XT:
+                product(i + 1, 1)
+            if there(i + 2):
+                reorder_pc(i + 2)
+            if there(i + 1):
+                quant_pf(i + 1)
             if there(i):
                 pool_out(i, 0)
             if there(i + 1):
-                product(i + 1, 0)
-                product(i + 1, 1)
-            if there(i - 1):
+                quant_pc(i + 1, 0, 4)
+            if there(i - 1) and i < NT:
                 quant_pooled(i - 1)
-            if there(i + 1):
-                quant_pc(i + 1, 0, 2)
-                quant_pc(i + 1, 2, 2)
-                quant_pf(i + 1)
-            if there(i):
-                s1_cached(i, 1)
-                s1_fresh(i, 1)
-            for h in range(2):
-                s2(i - 2, h)
-            if there(i + 2):
-                for g in range(GC):
-                    if i + 2 > 3:
-                        widen(i + 2, g, 1, nc.gpsimd.tensor_copy)
-                if i + 2 > 3:
-                    reorder_pf(i + 2)
-                    reorder_pc(i + 2)
-
         for i in range(2, NT + 1):
             period(i)
         for h in range(2):

@@ -66,7 +66,6 @@ def tile_pooled_sentence_embedding_s3_kernel(
             for j in range(n):
                 pfs[i + j] = t[:, j, :]
 
-        s_all = keep.tile([P, TC], F32, name="s_all", align_bytes=64)
         hcw = keep.tile([P, 2, GC, 2 * H], U8, name="hcw", align_bytes=64)
         ww = keep.tile([P, GD, 2 * E], U8, name="ww", align_bytes=64)
         hf_raw = keep.tile([P, GF, 2, 4, H], BF16, name="hf_raw", align_bytes=64)
@@ -93,31 +92,30 @@ def tile_pooled_sentence_embedding_s3_kernel(
                     in_=src[:, 4 * q : 4 * q + 4, :].rearrange("g q n -> q g n").bitcast(I32),
                 )
 
-        load_pc(1, 1)
-        nc.sync.dma_start(out=pc_sc[:], in_=pc_scale.rearrange("o (g p t) -> p (o g) t", p=P, t=4))
         load_pc(0, 1)
-        nc.sync.dma_start(out=inv_b[:], in_=inv_len.rearrange("(p i) -> p i", i=NT))
-        load_hf(0, 0)
-        load_hf(0, 1)
-        load_hf(1, 0)
-        load_pf(0, 1)
-        load_scales(hc_sc, hc_scales)
-        load_hc(0)
-        load_pf(3, 1)
-        load_pf(1, 1)
-        load_pf(2, 1)
-        load_hc(1)
         load_pc(2, 1)
+        nc.sync.dma_start(out=pc_sc[:], in_=pc_scale.rearrange("o (g p t) -> p (o g) t", p=P, t=4))
+        nc.sync.dma_start(out=inv_b[:], in_=inv_len.rearrange("(p i) -> p i", i=NT))
+        load_pf(0, 1)
+        load_pc(1, 1)
+        load_hf(0, 0)
+        load_pf(1, 1)
+        load_scales(hc_sc, hc_scales)
+        load_hf(1, 0)
+        load_hc(0)
         load_hf(1, 1)
-        load_pc(4, 2)
-        load_scales(w_sc, w_scales)
+        load_pf(2, 1)
         load_pc(3, 1)
-        nc.sync.dma_start(out=s_all[:], in_=pc_scale.rearrange("o k -> (o k)").partition_broadcast(P))
+        load_hf(0, 1)
+        load_hc(1)
+        load_pf(3, 1)
+        load_pc(4, 2)
         load_pf(4, 2)
+        load_scales(w_sc, w_scales)
         nc.sync.dma_start(out=ww[:], in_=w_words.rearrange("g p n -> p g n"))
-        nc.sync.dma_start(out=bias[:], in_=b.partition_broadcast(P))
-        load_pf(6, 2)
         load_pc(6, 2)
+        load_pf(6, 2)
+        nc.sync.dma_start(out=bias[:], in_=b.partition_broadcast(P))
 
         hfc = keep.tile([P, GF, D], U32, name="hfc", align_bytes=64)
         hfs = keep.tile([P, GF, D], U8, name="hfs", align_bytes=64)
@@ -150,31 +148,12 @@ def tile_pooled_sentence_embedding_s3_kernel(
             cols = slice(512 * g0, 512 * (g0 + n))
             engine(out=wide[i][:, cols], in_=pcb[i][:, cols].bitcast(FP8))
 
-        def scale_rows(i, g0, n):
-            if g0 == 0:
-                wide[i] = work.tile([P, TC], BF16, name="wide", tag="wide", bufs=3, align_bytes=64)
-            cols = slice(512 * g0, 512 * (g0 + n))
-            nc.vector.tensor_tensor(
-                out=wide[i][:, cols], in0=pcb[i][:, cols].bitcast(FP8), in1=s_all[:, cols], op=MULT
-            )
-
-        def reorder_pc(i):
-            t = work.tile([P, TC], BF16, name="pcr", tag="pcr", bufs=2, align_bytes=64)
-            pcr[i] = t
-            nc.vector.tensor_copy(
+        def reorder_pc(i, h, engine):
+            t = work.tile([P, TC // 2], BF16, name="pcr", tag=f"pcr{h}", bufs=2, align_bytes=64)
+            pcr[i, h] = t
+            engine(
                 out=t[:].bitcast(F32).rearrange("m (g u p) -> m g u p", u=2, p=P),
-                in_=wide[i][:].bitcast(F32).rearrange("m (g p u) -> m g u p", u=2, p=P),
-            )
-
-        def copy_pc(i, h):
-            if h == 0:
-                gpc[i] = work.tile([P, GC, P, 4], BF16, name="gpc", tag="gpc", align_bytes=64)
-            nc.scalar.copy(
-                out=gpc[i][:, 2 * h : 2 * h + 2, :, :]
-                .rearrange("p g r t -> p (g r t)")
-                .bitcast(F32)
-                .rearrange("p (g r u) -> p g r u", g=2, u=2),
-                in_=tpc[i, h][:].rearrange("p g u r -> p g r u"),
+                in_=wide[i][:, 1024 * h : 1024 * (h + 1)].bitcast(F32).rearrange("m (g p u) -> m g u p", u=2, p=P),
             )
 
         def keep_clock(n):
@@ -208,10 +187,13 @@ def tile_pooled_sentence_embedding_s3_kernel(
         def turn_pc(i, h):
             t = psum.tile([P, 2, 2, P], F32, name="tpc", tag=f"t{1 + h}")
             tpc[i, h] = t
-            plain = {i: wide[i][:]}
             for g in range(2):
                 for u in range(2):
-                    nc.tensor.transpose(t[:, g, u, :], words(i, pcr, plain, 2 * h + g, u), ident[:])
+                    nc.tensor.transpose(
+                        t[:, g, u, :],
+                        words((i, h), pcr, {(i, h): wide[i][:, 1024 * h : 1024 * (h + 1)]}, g, u),
+                        ident[:],
+                    )
 
         def product(i, h):
             if h == 0:
@@ -341,134 +323,145 @@ def tile_pooled_sentence_embedding_s3_kernel(
                 out=out.rearrange("(p i) e -> p i e", i=NT)[:, i, c0:c1], in_=zb[i][:, c0:c1]
             )
 
-        keep_clock(8)
-        widen(0, 0, 1, nc.vector.tensor_copy)
-        widen(0, 1, 1, nc.scalar.copy)
-        widen(0, 2, 1, nc.vector.tensor_copy)
-        turn_pc(0, 0)
-        keep_clock(4)
-        product(0, 0)
-        widen(1, 0, 2, nc.scalar.copy)
-        quant_pc(0, 0, 2)
+        widen(0, 0, 1, nc.scalar.copy)
+        keep_clock(5)
+        widen(0, 1, 1, nc.vector.tensor_copy)
         widen(0, 3, 1, nc.scalar.copy)
-        turn_pc(0, 1)
-        turn_pc(1, 0)
-        widen(1, 2, 2, nc.scalar.copy)
-        product(0, 1)
+        widen(1, 0, 2, nc.scalar.copy)
+        keep_clock(3)
+        turn_pc(0, 0)
+        hf_group(0, 0, nc.scalar.copy)
+        product(0, 0)
+        widen(0, 2, 1, nc.gpsimd.tensor_copy)
+        widen(2, 0, 1, nc.vector.tensor_copy)
         turn_pf(0)
-        product(1, 0)
-        hf_group(1, 0, nc.scalar.copy)
+        turn_pc(0, 1)
+        widen(1, 2, 2, nc.gpsimd.tensor_copy)
+        product(0, 1)
         copy_pf(0)
-        hf_group_gpsimd(0, 0)
-        turn_pc(1, 1)
+        hf_group(1, 0, nc.scalar.copy)
+        keep_clock(5)
+        quant_pc(0, 0, 2)
         quant_pc(0, 2, 2)
-        s1_cached(0, 0)
+        turn_pc(1, 1)
+        turn_pc(1, 0)
         turn_pf(1)
-        reorder_pf(3)
-        copy_pf(1)
-        hf_quant(1, 0)
-        nc.vector.tensor_copy(out=inv[:], in_=inv_b[:])
-        product(1, 1)
-        widen(2, 0, 2, nc.scalar.copy)
-        s1_cached(0, 1)
         hf_quant(0, 0)
-        quant_pf(0)
-        quant_pc(1, 0, 2)
+        copy_pf(1)
+        keep_clock(2)
+        widen(3, 0, 1, nc.scalar.copy)
+        s1_cached(0, 0)
         hf_group(1, 1, nc.scalar.copy)
-        quant_pc(1, 2, 2)
-        turn_pf(2)
-        quant_pf(1)
-        widen(2, 2, 2, nc.vector.tensor_copy)
-        widen(3, 0, 2, nc.scalar.copy)
+        widen(2, 1, 1, nc.gpsimd.tensor_copy)
+        product(1, 0)
+        product(1, 1)
+        widen(2, 2, 1, nc.gpsimd.tensor_copy)
+        widen(3, 3, 1, nc.vector.tensor_copy)
         turn_pc(2, 0)
-        turn_pc(2, 1)
+        turn_pf(2)
+        reorder_pf(3)
+        hf_quant(1, 0)
+        quant_pc(1, 0, 2)
+        widen(2, 3, 1, nc.vector.tensor_copy)
+        nc.vector.tensor_copy(out=inv[:], in_=inv_b[:])
+        quant_pc(1, 2, 2)
+        widen(4, 0, 1, nc.scalar.copy)
         hf_group(0, 1, nc.vector.tensor_copy)
-        product(2, 0)
-        s1_cached(1, 1)
-        hf_quant(0, 1)
+        quant_pf(1)
+        s1_cached(1, 0)
+        quant_pf(0)
+        s1_cached(0, 1)
+        widen(3, 2, 1, nc.scalar.copy)
+        turn_pc(2, 1)
         s1_fresh(0, 0)
         copy_pf(2)
+        hf_quant(0, 1)
         hf_quant(1, 1)
-        quant_pc(2, 0, 2)
+        product(2, 0)
         product(2, 1)
-        widen(3, 2, 2, nc.vector.tensor_copy)
-        s1_cached(1, 0)
         pool_out(0, 0)
         s1_fresh(0, 1)
-        quant_pc(2, 2, 2)
         s1_fresh(1, 0)
+        widen(3, 1, 1, nc.vector.tensor_copy)
+        s1_cached(1, 1)
+        quant_pc(2, 0, 2)
+        reorder_pc(3, 0, nc.vector.tensor_copy)
         pool_out(0, 1)
-        s1_fresh(1, 1)
+        reorder_pc(3, 1, nc.scalar.copy)
+        widen(4, 2, 1, nc.vector.tensor_copy)
+        quant_pc(2, 2, 2)
         turn_pooled(0)
-        quant_pf(2)
+        s1_fresh(1, 1)
         pool_out(1, 0)
+        widen(4, 3, 1, nc.vector.tensor_copy)
         copy_pooled(0)
+        quant_pf(2)
         quant_pooled(0)
+        widen(4, 1, 1, nc.vector.tensor_copy)
         def there(i):
             return 0 <= i < NT
 
         def period(i):
             if there(i - 1):
                 pool_out(i - 1, 1)
-            if there(i + 1):
-                turn_pc(i + 1, 1)
-            if there(i + 1):
-                turn_pc(i + 1, 0)
-            if there(i + 1):
-                turn_pf(i + 1)
-            if there(i + 1) and i + 1 >= XT:
-                copy_pc(i + 1, 0)
             if there(i - 3):
                 add_bias(i - 3, 0)
                 tanh(i - 3, 0)
+            if there(i + 1):
+                turn_pc(i + 1, 0)
+            if there(i + 1):
+                turn_pc(i + 1, 1)
+            if there(i + 1):
+                turn_pf(i + 1)
             if there(i - 1) and i < NT:
                 turn_pooled(i - 1)
-            if there(i - 1) and i < NT:
-                copy_pooled(i - 1)
-            if i + 1 < XT:
+            if there(i + 1):
                 product(i + 1, 0)
-            if there(i + 2):
-                scale_rows(i + 2, 0, 2)
-            if there(i):
-                s1_cached(i, 1)
+            if 4 <= i + 2 < NT:
+                reorder_pc(i + 2, 0, nc.vector.tensor_copy)
+            if there(i + 1):
+                product(i + 1, 1)
             if there(i + 1):
                 copy_pf(i + 1)
+            if there(i + 1):
+                quant_pc(i + 1, 0, 2)
+            if there(i):
+                s1_cached(i, 0)
+            if there(i - 1) and i < NT:
+                copy_pooled(i - 1)
+            if there(i):
+                s1_fresh(i, 0)
+            if there(i):
+                s1_cached(i, 1)
+            if there(i + 3) and i + 3 >= 5:
+                for g in range(GC):
+                    widen(i + 3, g, 1, nc.gpsimd.tensor_copy)
+            if there(i):
+                pool_out(i, 0)
+            if there(i + 2):
+                reorder_pf(i + 2)
+            if there(i):
+                s1_fresh(i, 1)
             if there(i - 3):
                 add_bias(i - 3, 1)
                 tanh(i - 3, 1)
                 store(i - 3, 0, E)
-            if there(i):
-                s1_cached(i, 0)
+            if there(i - 2):
+                s2(i - 2, 0)
             if i == NT:
                 turn_pooled(i - 1)
                 copy_pooled(i - 1)
                 quant_pooled(i - 1)
-            if there(i):
-                s1_fresh(i, 0)
-            if there(i + 2):
-                reorder_pf(i + 2)
-            if there(i + 2):
-                scale_rows(i + 2, 2, 2)
-            if there(i):
-                s1_fresh(i, 1)
-            if there(i - 2):
-                s2(i - 2, 0)
-            if there(i - 2):
-                s2(i - 2, 1)
-            if there(i + 1) and i + 1 >= XT:
-                copy_pc(i + 1, 1)
-            if i + 1 < XT:
-                product(i + 1, 1)
-            if there(i + 2):
-                reorder_pc(i + 2)
-            if there(i + 1):
-                quant_pf(i + 1)
-            if there(i):
-                pool_out(i, 0)
-            if there(i + 1):
-                quant_pc(i + 1, 0, 4)
             if there(i - 1) and i < NT:
                 quant_pooled(i - 1)
+            if 4 <= i + 2 < NT:
+                reorder_pc(i + 2, 1, nc.scalar.copy)
+            if there(i + 1):
+                quant_pf(i + 1)
+            if there(i - 2):
+                s2(i - 2, 1)
+            if there(i + 1):
+                quant_pc(i + 1, 2, 2)
         for i in range(2, NT + 1):
             period(i)
         for h in range(2):

from contextlib import ExitStack

import concourse.mybir as mybir
from concourse.masks import make_identity

M, TF, TC, D, E = 1024, 1024, 2048, 1024, 1024
FLOPS = 2 * M * D * (TF + TC) + 2 * M * D * E

F32 = mybir.dt.float32
BF16 = mybir.dt.bfloat16
I32 = mybir.dt.int32
U32 = mybir.dt.uint32
U8 = mybir.dt.uint8
FP8 = mybir.dt.float8_e4m3fn
FP8X4 = mybir.dt.float8_e4m3fn_x4
FP4X4 = mybir.dt.float4_e2m1fn_x4
COPY = mybir.ActivationFunctionType.Copy
TANH = mybir.ActivationFunctionType.Tanh
MULT = mybir.AluOpType.mult
ADD = mybir.AluOpType.add

P = 128
NT = M // P
GF = TF // 512
GC = TC // 512
GD = D // 512
H = 512
XT = 4


def tile_pooled_sentence_embedding_s3_kernel(
    tc, pf, hf, pc_bytes, pc_scale, hc_words, hc_scales, inv_len, w_words, w_scales, b, out
):
    nc = tc.nc
    with ExitStack() as ctx:
        keep = ctx.enter_context(tc.tile_pool(name="keep", bufs=1))
        work = ctx.enter_context(tc.tile_pool(name="work", bufs=2))
        psum = ctx.enter_context(tc.psum_pool(name="psum", bufs=1))
        ctx.enter_context(tc.manual_schedule())

        ident = keep.tile([P, P], F32, name="ident", align_bytes=64)
        pc_sc = keep.tile([P, GC, 4], F32, name="pc_sc", align_bytes=64)
        hc_sc = keep.tile([P, GC, D], U8, name="hc_sc", align_bytes=64)
        w_sc = keep.tile([P, GD, E], U8, name="w_sc", align_bytes=64)
        warm = keep.tile([P, 2], F32, name="warm", align_bytes=64)
        nc.vector.memset(warm[:], 0.0)
        idle = keep.tile([P, H], BF16, name="idle", align_bytes=64)
        nc.gpsimd.memset(idle[:], 0.0)
        nc.vector.memset(hc_sc[:].rearrange("p g n -> p (g n)").bitcast(I32), 0)
        nc.vector.memset(w_sc[:].rearrange("p g n -> p (g n)").bitcast(I32), 0)
        nc.scalar.activation(out=warm[:, 0:1], in_=warm[:, 1:2], func=TANH)
        make_identity(nc, ident[:])

        pcb = {}
        pfs = {}

        def load_pc(i, n):
            t = keep.tile([P, n, TC], U8, name=f"pcb{i}", tag=f"pcb{i}", align_bytes=64)
            nc.sync.dma_start(out=t[:], in_=pc_bytes.rearrange("(p i) k -> p i k", i=NT)[:, i : i + n, :])
            for j in range(n):
                pcb[i + j] = t[:, j, :]

        def load_pf(i, n):
            t = keep.tile([P, n, TF], BF16, name=f"pfs{i}", tag=f"pfs{i}", align_bytes=64)
            nc.sync.dma_start(out=t[:], in_=pf.rearrange("(p i) k -> p i k", i=NT)[:, i : i + n, :])
            for j in range(n):
                pfs[i + j] = t[:, j, :]

        hcw = keep.tile([P, 2, GC, 2 * H], U8, name="hcw", align_bytes=64)
        ww = keep.tile([P, GD, 2 * E], U8, name="ww", align_bytes=64)
        hf_raw = keep.tile([P, GF, 2, 4, H], BF16, name="hf_raw", align_bytes=64)
        inv_b = keep.tile([P, NT], BF16, name="inv_b", align_bytes=64)
        inv = keep.tile([P, NT], F32, name="inv", align_bytes=64)
        bias = keep.tile([P, E], BF16, name="bias", align_bytes=64)

        def load_hc(h):
            nc.sync.dma_start(
                out=hcw[:, h, :, :],
                in_=hc_words.rearrange("g p n -> p g n")[:, :, 2 * H * h : 2 * H * (h + 1)],
            )

        def load_hf(g, h):
            nc.sync.dma_start(
                out=hf_raw[:, g, h, :, :],
                in_=hf.rearrange("(g p t) d -> g p t d", p=P, t=4)[g, :, :, H * h : H * (h + 1)],
            )

        def load_scales(tile, src):
            for q in range(4):
                nc.sync.dma_start(
                    out=tile[32 * q : 32 * q + 4, :, :].bitcast(I32),
                    in_=src[:, 4 * q : 4 * q + 4, :].rearrange("g q n -> q g n").bitcast(I32),
                )

        load_pc(0, 1)
        load_pc(2, 1)
        nc.sync.dma_start(out=pc_sc[:], in_=pc_scale.rearrange("o (g p t) -> p (o g) t", p=P, t=4))
        nc.sync.dma_start(out=inv_b[:], in_=inv_len.rearrange("(p i) -> p i", i=NT))
        load_pf(0, 1)
        load_pc(1, 1)
        load_hf(0, 0)
        load_pf(1, 1)
        load_scales(hc_sc, hc_scales)
        load_hf(1, 0)
        load_hc(0)
        load_hf(1, 1)
        load_pf(2, 1)
        load_pc(3, 1)
        load_hf(0, 1)
        load_hc(1)
        load_pf(3, 1)
        load_pc(4, 2)
        load_pf(4, 2)
        load_scales(w_sc, w_scales)
        nc.sync.dma_start(out=ww[:], in_=w_words.rearrange("g p n -> p g n"))
        load_pc(6, 2)
        load_pf(6, 2)
        nc.sync.dma_start(out=bias[:], in_=b.partition_broadcast(P))

        hfc = keep.tile([P, GF, D], U32, name="hfc", align_bytes=64)
        hfs = keep.tile([P, GF, D], U8, name="hfs", align_bytes=64)
        hfg = {}
        wide, pcr, pfr = {}, {}, {}
        tpc, gpc, qc, qs = {}, {}, {}, {}
        tpf, gpf, fc, fs = {}, {}, {}, {}
        acc, pooled, tpo, gpo, oc, os_ = {}, {}, {}, {}, {}, {}
        zac, zb = {}, {}

        def hf_group(g, h, engine):
            t = work.tile([P, H, 4], BF16, name="hfg", tag=f"hfg{g}", align_bytes=64)
            hfg[g, h] = t
            engine(
                out=t[:].rearrange("p (c i) t -> p c t i", i=4),
                in_=hf_raw[:, g, h, :, :].rearrange("p t (c i) -> p c t i", i=4),
            )

        def hf_quant(g, h):
            cols = slice(H * h, H * (h + 1))
            nc.vector.quantize_mx(
                out=hfc[:, g, cols].bitcast(FP8X4),
                scales=hfs[:, g, cols],
                in_=hfg[g, h][:].rearrange("p c t -> p (c t)"),
            )

        def widen(i, g0, n, engine):
            if g0 == 0:
                wide[i] = work.tile([P, TC], BF16, name="wide", tag="wide", bufs=3, align_bytes=64)
            cols = slice(512 * g0, 512 * (g0 + n))
            engine(out=wide[i][:, cols], in_=pcb[i][:, cols].bitcast(FP8))

        def reorder_pc(i, h, engine):
            t = work.tile([P, TC // 2], BF16, name="pcr", tag=f"pcr{h}", bufs=2, align_bytes=64)
            pcr[i, h] = t
            engine(
                out=t[:].bitcast(F32).rearrange("m (g u p) -> m g u p", u=2, p=P),
                in_=wide[i][:, 1024 * h : 1024 * (h + 1)].bitcast(F32).rearrange("m (g p u) -> m g u p", u=2, p=P),
            )

        def keep_clock(n):
            t = psum.tile([P, H], F32, name="clock", tag="t3")
            for j in range(n):
                nc.tensor.matmul(t[:], idle[:, 0:P], idle[:], start=True, stop=True)

        def hf_group_gpsimd(g, h):
            t = work.tile([P, H, 4], BF16, name="hfg", tag=f"hfg{g}", align_bytes=64)
            hfg[g, h] = t
            for c in range(4):
                nc.gpsimd.tensor_scalar(
                    t[:, P * c : P * (c + 1), :],
                    hf_raw[:, g, h, :, P * c : P * (c + 1)].rearrange("p t d -> p d t"),
                    1.0, 0.0, MULT, ADD,
                )

        def reorder_pf(i):
            t = work.tile([P, TF], BF16, name="pfr", tag="pfr", bufs=2, align_bytes=64)
            pfr[i] = t
            nc.scalar.copy(
                out=t[:].bitcast(F32).rearrange("m (g u p) -> m g u p", u=2, p=P),
                in_=pfs[i].bitcast(F32).rearrange("m (g p u) -> m g u p", u=2, p=P),
            )

        def words(i, ordered, plain, g, u):
            if i in ordered:
                return ordered[i][:].bitcast(F32)[:, 256 * g + 128 * u : 256 * g + 128 * (u + 1)]
            return plain[i].bitcast(F32)[:, 256 * g + u : 256 * (g + 1) : 2]

        def turn_pc(i, h):
            t = psum.tile([P, 2, 2, P], F32, name="tpc", tag=f"t{1 + h}")
            tpc[i, h] = t
            for g in range(2):
                for u in range(2):
                    nc.tensor.transpose(
                        t[:, g, u, :],
                        words((i, h), pcr, {(i, h): wide[i][:, 1024 * h : 1024 * (h + 1)]}, g, u),
                        ident[:],
                    )

        def product(i, h):
            if h == 0:
                gpc[i] = work.tile([P, GC, P, 4], BF16, name="gpc", tag="gpc", align_bytes=64)
            for j in range(2):
                g = 2 * h + j
                nc.vector.tensor_tensor(
                    out=gpc[i][:, g, :, :].rearrange("p r (u e) -> p r u e", u=2),
                    in0=tpc[i, h][:, j, :, :].bitcast(BF16).rearrange("p u (r e) -> p r u e", e=2),
                    in1=pc_sc[:, g, :].rearrange("p (u e) -> p u e", u=2).unsqueeze(1).to_broadcast([P, P, 2, 2]),
                    op=MULT,
                )

        def quant_pc(i, g0, n):
            if g0 == 0:
                qc[i] = work.tile([P, GC * P], U32, name="qc", tag="qc", align_bytes=64)
                qs[i] = work.tile([P, GC * P], U8, name="qs", tag="qs", align_bytes=64)
            cols = slice(P * g0, P * (g0 + n))
            nc.vector.quantize_mx(
                out=qc[i][:, cols].bitcast(FP8X4),
                scales=qs[i][:, cols],
                in_=gpc[i][:, g0 : g0 + n, :, :].rearrange("p g r t -> p (g r t)"),
            )

        def turn_pf(i):
            t = psum.tile([P, GF, 2, P], F32, name="tpf", tag="t0")
            tpf[i] = t
            for g in range(GF):
                for u in range(2):
                    nc.tensor.transpose(t[:, g, u, :], words(i, pfr, pfs, g, u), ident[:])

        def copy_pf(i):
            gpf[i] = work.tile([P, GF * P * 4], BF16, name="gpf", tag="gpf", align_bytes=64)
            nc.scalar.copy(
                out=gpf[i][:].bitcast(F32).rearrange("p (g r u) -> p g r u", g=GF, u=2),
                in_=tpf[i][:].rearrange("p g u r -> p g r u"),
            )

        def quant_pf(i):
            fc[i] = work.tile([P, GF * P], U32, name="fc", tag="fc", align_bytes=64)
            fs[i] = work.tile([P, GF * P], U8, name="fs", tag="fs", align_bytes=64)
            nc.vector.quantize_mx(out=fc[i][:].bitcast(FP8X4), scales=fs[i][:], in_=gpf[i][:])

        def s1_cached(i, h):
            acc[i, h] = psum.tile([P, H], F32, name="acc", tag="acc", bufs=4)
            for g in range(GC):
                rows = slice(P * g, P * (g + 1))
                nc.tensor.matmul_mx(
                    out=acc[i, h][:],
                    lhsT=qc[i][:, rows].bitcast(FP8X4),
                    lhsT_scale=qs[i][:, rows],
                    rhs=hcw[:, h, g, :].bitcast(FP4X4),
                    rhs_scale=hc_sc[:, g, H * h : H * (h + 1)],
                    start=(g == 0),
                    stop=False,
                )

        def s1_fresh(i, h):
            for g in range(GF):
                rows = slice(P * g, P * (g + 1))
                nc.tensor.matmul_mx(
                    out=acc[i, h][:],
                    lhsT=fc[i][:, rows].bitcast(FP8X4),
                    lhsT_scale=fs[i][:, rows],
                    rhs=hfc[:, g, H * h : H * (h + 1)].bitcast(FP8X4),
                    rhs_scale=hfs[:, g, H * h : H * (h + 1)],
                    start=False,
                    stop=(g == GF - 1),
                )

        def pool_out(i, h):
            if h == 0:
                pooled[i] = work.tile([P, D], BF16, name="pooled", tag="pooled", align_bytes=64)
            nc.scalar.activation(
                out=pooled[i][:, H * h : H * (h + 1)].rearrange("m (u p e) -> m u p e", u=2, e=2),
                in_=acc[i, h][:].rearrange("m (p u e) -> m u p e", u=2, e=2),
                func=COPY,
                scale=inv[:, i : i + 1],
            )

        def turn_pooled(i):
            t = psum.tile([P, GD, 2, P], F32, name="tpo", tag="t3")
            tpo[i] = t
            w = pooled[i][:].bitcast(F32)
            for g in range(GD):
                for u in range(2):
                    nc.tensor.transpose(t[:, g, u, :], w[:, 256 * g + 128 * u : 256 * g + 128 * (u + 1)], ident[:])

        def copy_pooled(i):
            gpo[i] = work.tile([P, GD * P * 4], BF16, name="gpo", tag="gpo", align_bytes=64)
            nc.scalar.copy(
                out=gpo[i][:].bitcast(F32).rearrange("p (g r u) -> p g r u", g=GD, u=2),
                in_=tpo[i][:].rearrange("p g u r -> p g r u"),
            )

        def quant_pooled(i):
            oc[i] = work.tile([P, GD * P], U32, name="oc", tag="oc", align_bytes=64)
            os_[i] = work.tile([P, GD * P], U8, name="os", tag="os", align_bytes=64)
            nc.vector.quantize_mx(out=oc[i][:].bitcast(FP8X4), scales=os_[i][:], in_=gpo[i][:])

        def s2(i, h):
            zac[i, h] = psum.tile([P, H], F32, name="zac", tag="acc", bufs=4)
            for g in range(GD):
                rows = slice(P * g, P * (g + 1))
                nc.tensor.matmul_mx(
                    out=zac[i, h][:],
                    lhsT=oc[i][:, rows].bitcast(FP8X4),
                    lhsT_scale=os_[i][:, rows],
                    rhs=ww[:, g, 2 * H * h : 2 * H * (h + 1)].bitcast(FP4X4),
                    rhs_scale=w_sc[:, g, H * h : H * (h + 1)],
                    start=(g == 0),
                    stop=(g == GD - 1),
                )

        def add_bias(i, h):
            if h == 0:
                zb[i] = work.tile([P, E], F32, name="zb", tag="zb", bufs=3, align_bytes=64)
            cols = slice(H * h, H * (h + 1))
            nc.vector.tensor_tensor(out=zb[i][:, cols], in0=zac[i, h][:], in1=bias[:, cols], op=ADD)

        def tanh(i, h):
            cols = slice(H * h, H * (h + 1))
            nc.scalar.activation(out=zb[i][:, cols], in_=zb[i][:, cols], func=TANH)

        def store(i, c0, c1):
            nc.sync.dma_start(
                out=out.rearrange("(p i) e -> p i e", i=NT)[:, i, c0:c1], in_=zb[i][:, c0:c1]
            )

        widen(0, 0, 1, nc.scalar.copy)
        keep_clock(5)
        widen(0, 1, 1, nc.vector.tensor_copy)
        widen(0, 3, 1, nc.scalar.copy)
        widen(1, 0, 2, nc.scalar.copy)
        keep_clock(3)
        turn_pc(0, 0)
        hf_group(0, 0, nc.scalar.copy)
        product(0, 0)
        widen(0, 2, 1, nc.gpsimd.tensor_copy)
        widen(2, 0, 1, nc.vector.tensor_copy)
        turn_pf(0)
        turn_pc(0, 1)
        widen(1, 2, 2, nc.gpsimd.tensor_copy)
        product(0, 1)
        copy_pf(0)
        hf_group(1, 0, nc.scalar.copy)
        keep_clock(5)
        quant_pc(0, 0, 2)
        quant_pc(0, 2, 2)
        turn_pc(1, 1)
        turn_pc(1, 0)
        turn_pf(1)
        hf_quant(0, 0)
        copy_pf(1)
        keep_clock(2)
        widen(3, 0, 1, nc.scalar.copy)
        s1_cached(0, 0)
        hf_group(1, 1, nc.scalar.copy)
        widen(2, 1, 1, nc.gpsimd.tensor_copy)
        product(1, 0)
        product(1, 1)
        widen(2, 2, 1, nc.gpsimd.tensor_copy)
        widen(3, 3, 1, nc.vector.tensor_copy)
        turn_pc(2, 0)
        turn_pf(2)
        reorder_pf(3)
        hf_quant(1, 0)
        quant_pc(1, 0, 2)
        widen(2, 3, 1, nc.vector.tensor_copy)
        nc.vector.tensor_copy(out=inv[:], in_=inv_b[:])
        quant_pc(1, 2, 2)
        widen(4, 0, 1, nc.scalar.copy)
        hf_group(0, 1, nc.vector.tensor_copy)
        quant_pf(1)
        s1_cached(1, 0)
        quant_pf(0)
        s1_cached(0, 1)
        widen(3, 2, 1, nc.scalar.copy)
        turn_pc(2, 1)
        s1_fresh(0, 0)
        copy_pf(2)
        hf_quant(0, 1)
        hf_quant(1, 1)
        product(2, 0)
        product(2, 1)
        pool_out(0, 0)
        s1_fresh(0, 1)
        s1_fresh(1, 0)
        widen(3, 1, 1, nc.vector.tensor_copy)
        s1_cached(1, 1)
        quant_pc(2, 0, 2)
        reorder_pc(3, 0, nc.vector.tensor_copy)
        pool_out(0, 1)
        reorder_pc(3, 1, nc.scalar.copy)
        widen(4, 2, 1, nc.vector.tensor_copy)
        quant_pc(2, 2, 2)
        turn_pooled(0)
        s1_fresh(1, 1)
        pool_out(1, 0)
        widen(4, 3, 1, nc.vector.tensor_copy)
        copy_pooled(0)
        quant_pf(2)
        quant_pooled(0)
        widen(4, 1, 1, nc.vector.tensor_copy)
        def there(i):
            return 0 <= i < NT

        def period(i):
            if there(i - 1):
                pool_out(i - 1, 1)
            if there(i - 3):
                add_bias(i - 3, 0)
                tanh(i - 3, 0)
            if there(i + 1):
                turn_pc(i + 1, 0)
            if there(i + 1):
                turn_pc(i + 1, 1)
            if there(i + 1):
                turn_pf(i + 1)
            if there(i - 1) and i < NT:
                turn_pooled(i - 1)
            if there(i + 1):
                product(i + 1, 0)
            if 4 <= i + 2 < NT:
                reorder_pc(i + 2, 0, nc.vector.tensor_copy)
            if there(i + 1):
                product(i + 1, 1)
            if there(i + 1):
                copy_pf(i + 1)
            if there(i + 1):
                quant_pc(i + 1, 0, 2)
            if there(i):
                s1_cached(i, 0)
            if there(i - 1) and i < NT:
                copy_pooled(i - 1)
            if there(i):
                s1_fresh(i, 0)
            if there(i):
                s1_cached(i, 1)
            if there(i + 3) and i + 3 >= 5:
                for g in range(GC):
                    widen(i + 3, g, 1, nc.gpsimd.tensor_copy)
            if there(i):
                pool_out(i, 0)
            if there(i + 2):
                reorder_pf(i + 2)
            if there(i):
                s1_fresh(i, 1)
            if there(i - 3):
                add_bias(i - 3, 1)
                tanh(i - 3, 1)
                store(i - 3, 0, E)
            if there(i - 2):
                s2(i - 2, 0)
            if i == NT:
                turn_pooled(i - 1)
                copy_pooled(i - 1)
                quant_pooled(i - 1)
            if there(i - 1) and i < NT:
                quant_pooled(i - 1)
            if 4 <= i + 2 < NT:
                reorder_pc(i + 2, 1, nc.scalar.copy)
            if there(i + 1):
                quant_pf(i + 1)
            if there(i - 2):
                s2(i - 2, 1)
            if there(i + 1):
                quant_pc(i + 1, 2, 2)
        for i in range(2, NT + 1):
            period(i)
        for h in range(2):
            s2(NT - 1, h)
        for i in (NT - 2, NT - 1):
            for h in range(2):
                add_bias(i, h)
                tanh(i, h)
                store(i, H * h, H * (h + 1))
